import numpy as np
import ml_dtypes


def mxq(x, axis, fmt="e4m3"):
    dtype, down = {"e4m3": (ml_dtypes.float8_e4m3fn, 7), "e5m2": (ml_dtypes.float8_e5m2, 14)}[fmt]
    v = np.moveaxis(np.asarray(x, np.float32).astype(ml_dtypes.bfloat16).astype(np.float64), axis, -1)
    blocks = v.reshape(v.shape[:-1] + (-1, 32))
    amax = np.abs(blocks).max(-1, keepdims=True)
    byte = np.maximum(np.where(amax > 0, np.frexp(amax)[1] - 1 + 127, 0) - down, 1)
    scale = np.exp2(byte - 127.0)
    codes = (blocks / scale).astype(np.float32).astype(dtype).astype(np.float64)
    return np.moveaxis((codes * scale).reshape(v.shape), -1, axis)


WIDE = False


def mx_kscale(k):
    if not WIDE:
        return np.ones(k)
    levels = np.array([10, -10, 5, -5, 0])
    if k % 512:
        return np.exp2(np.random.permutation(np.resize(levels, k // 32))).repeat(32)
    a = np.empty((k // 512, 16))
    for p in range(k // 512):
        a[p, :8] = np.random.permutation(np.resize(levels, 8))
        for g in range(8):
            far = levels[np.abs(levels - a[p, g]) >= 10]
            a[p, g + 8] = far[np.random.randint(len(far))]
    return np.exp2(a.ravel()).repeat(32)


def f64(x):
    return np.asarray(x).astype(np.float64)


def striped(idx):
    return np.tile(idx.reshape(-1, 16).T, (8, 1)).astype(np.uint16)


def unstriped(offs):
    return offs[:16].T.reshape(-1).astype(np.int64)


E2M1 = np.array([0.0, 0.5, 1.0, 1.5, 2.0, 3.0, 4.0, 6.0, -0.0, -0.5, -1.0, -1.5, -2.0, -3.0, -4.0, -6.0])


def pack_weight(w, fmt):
    k, n = w.shape
    w = f64(np.asarray(w, np.float32).astype(ml_dtypes.bfloat16)).reshape(k // 32, 32, n)
    amax = np.abs(w).max(1)
    if fmt == "e4m3":
        byte = np.frexp(amax)[1] - 1 + 127 - 7
    else:
        mant, ex = np.frexp(amax / 6.0)
        byte = np.where(mant > 0.5, ex, ex - 1) + 127
    byte = np.clip(np.where(amax > 0, byte, 1), 1, 254)
    scaled = (w * np.exp2(127.0 - byte)[:, None, :]).reshape(k, n).astype(np.float32)
    by_word = np.ascontiguousarray(scaled.reshape(k // 512, 128, 4, n).transpose(0, 1, 3, 2))
    if fmt == "e4m3":
        words = by_word.astype(ml_dtypes.float8_e4m3fn).view(np.uint8)
    else:
        c = by_word.astype(ml_dtypes.float4_e2m1fn).view(np.uint8) & 0xF
        words = (c[..., 0::2] | (c[..., 1::2] << 4)).reshape(k // 512, 128, 2 * n)
    return np.ascontiguousarray(words), np.ascontiguousarray(byte.astype(np.uint8).reshape(k // 512, 16, n))


def unpack_weight(words, scales, fmt):
    g, _, n = scales.shape
    words = np.ascontiguousarray(words).reshape(g, 128, n, -1)
    if fmt == "e4m3":
        vals = words.view(ml_dtypes.float8_e4m3fn).astype(np.float64)
    else:
        nib = np.empty((g, 128, n, 4), np.uint8)
        nib[..., 0::2] = words & 0xF
        nib[..., 1::2] = words >> 4
        vals = E2M1[nib]
    vals = vals * np.repeat(np.exp2(scales.astype(np.float64) - 127.0), 8, axis=1)[..., None]
    return vals.transpose(0, 1, 3, 2).reshape(g * 512, n)


def pack_table(v):
    words, scales = pack_weight(v, "e4m3")
    return np.concatenate([words.reshape(words.shape[0], -1), scales.reshape(scales.shape[0], -1)], axis=1)


def unpack_table(tab):
    g, t = tab.shape[0], tab.shape[1] // 528
    return unpack_weight(tab[:, :512 * t].reshape(g, 128, t, 4), tab[:, 512 * t:].reshape(g, 16, t), "e4m3")


def silu(v):
    return v / (1.0 + np.exp(-np.maximum(v, -700.0)))


G, K, M, T, S = 2, 512, 256, 4096, 1024


def setup_inputs():
    n = np.random.standard_normal
    s = mx_kscale(K)[:, None]
    p_w4 = pack_weight(n((K, M)) / np.sqrt(K) / s, "e2m1")
    return {
        "tab": pack_table(n((K, T)) * s),
        "w4_words": p_w4[0],
        "w4_scales": p_w4[1],
        "dw": (0.3 * n((K, M)) / np.sqrt(K) / s).astype(np.float32),
        "b": (0.3 * n(256)).astype(np.float32),
        "offs": striped(np.concatenate([np.random.permutation(T)[:S] for _ in range(G)])),
    }


def reference(tab, w4_words, w4_scales, dw, b, offs):
    tab_ = unpack_table(tab)[:, unstriped(offs).reshape(G, S)].sum(1)
    w4_ = unpack_weight(w4_words, w4_scales, "e2m1")
    dw_ = mxq(f64(dw), 0, "e4m3")
    y = w4_.T @ tab_ + dw_.T @ tab_
    return silu(y + f64(b)[:, None])

@@ -1,0 +1,120 @@
+from contextlib import ExitStack
+
+import concourse.mybir as mybir
+
+G, K, M, T, S = 2, 512, 256, 4096, 1024
+FLOPS = 2 * 2 * G * K * M * S
+
+F32 = mybir.dt.float32
+BF16 = mybir.dt.bfloat16
+I32 = mybir.dt.int32
+U32 = mybir.dt.uint32
+U16 = mybir.dt.uint16
+U8 = mybir.dt.uint8
+FP8X4 = mybir.dt.float8_e4m3fn_x4
+FP4X4 = mybir.dt.float4_e2m1fn_x4
+SILU = mybir.ActivationFunctionType.Silu
+
+P = 128
+PACK = 4
+N = 512
+LANES = 16
+BLOCKS = 16
+TOP = P - BLOCKS
+
+
+def tile_list_tabbag_sum_silu_kernel(tc, tab, w4_words, w4_scales, dw, b, offs, out):
+    nc = tc.nc
+    with ExitStack() as ctx:
+        keep = ctx.enter_context(tc.tile_pool(name="keep", bufs=1))
+        psum = ctx.enter_context(tc.psum_pool(name="psum", bufs=1))
+
+        offsets = keep.tile([P, G * S // LANES], U16, name="offsets")
+        table_words = keep.tile([P, T], U32, name="table_words", align_bytes=64)
+        table_scales = keep.tile([P, T], U8, name="table_scales", align_bytes=64)
+        w4_codes = keep.tile([P, 2 * M], U8, name="w4_codes", align_bytes=64)
+        w4_plane = keep.tile([P, M], U8, name="w4_plane", align_bytes=64)
+        dw_raw = keep.tile([P, PACK, M], F32, name="dw_raw", align_bytes=64)
+        bias = keep.tile([P, M // P], F32, name="bias")
+        planes = [keep.tile([P, S], U8, name="plane%d" % g, align_bytes=64) for g in range(G)]
+
+        nc.vector.memset(w4_plane[:].bitcast(I32), 0)
+        nc.vector.memset(table_scales[0:TOP, :].bitcast(I32), 0)
+        for g in range(G):
+            nc.vector.memset(planes[g][:].bitcast(I32), 0)
+
+        nc.sync.dma_start(offsets[:], offs)
+        nc.scalar.dma_start(
+            table_scales[TOP:P, :].bitcast(I32),
+            tab[0, 512 * T : 528 * T].rearrange("(q t) -> q t", q=BLOCKS).bitcast(I32),
+        )
+        nc.sync.dma_start(
+            table_words[:].bitcast(I32), tab[0, 0 : 512 * T].rearrange("(p t) -> p t", p=P).bitcast(I32)
+        )
+        for q in range(4):
+            nc.scalar.dma_start(
+                w4_plane[32 * q : 32 * q + 4, :].bitcast(I32), w4_scales[0, 4 * q : 4 * q + 4, :].bitcast(I32)
+            )
+        nc.sync.dma_start(w4_codes[:].bitcast(I32), w4_words[0].bitcast(I32))
+        with nc.allow_non_contiguous_dma(reason="one bias value to a partition"):
+            nc.sync.dma_start(bias[:], b.rearrange("(c p) -> p c", p=P))
+        nc.sync.dma_start(dw_raw[:], dw.rearrange("(p j) n -> p j n", j=PACK))
+
+        for g, queue in enumerate((nc.scalar, nc.sync)):
+            picked = keep.tile([P, S], U8, name="picked_scales%d" % g, align_bytes=64)
+            cols = slice(g * S // LANES, (g + 1) * S // LANES)
+            nc.vector.tensor_copy(picked[:], table_scales[:].indirect(offsets[:, cols]))
+            for q in range(4):
+                queue.dma_start(
+                    planes[g][32 * q : 32 * q + 4, :].bitcast(I32),
+                    picked[TOP + 4 * q : TOP + 4 * q + 4, :].bitcast(I32),
+                )
+
+        def gather_words(g, h, tag):
+            picked = keep.tile([P, N], U32, name="picked_words%d%d" % (g, h), tag=tag, align_bytes=64)
+            first = (g * S + h * N) // LANES
+            nc.vector.tensor_copy(picked[:], table_words[:].indirect(offsets[:, first : first + N // LANES]))
+            return picked
+
+        banks = [[psum.tile([P, N], F32, name="bank%d%d" % (h, m)) for m in range(2)] for h in range(2)]
+
+        def multiply(words, g, h, m, codes, plane, start, stop):
+            nc.tensor.matmul_mx(
+                out=banks[h][m][:],
+                lhsT=codes,
+                lhsT_scale=plane,
+                rhs=words[:].bitcast(FP8X4),
+                rhs_scale=planes[g][:, h * N : (h + 1) * N],
+                start=start,
+                stop=stop,
+            )
+
+        def w4_operand(m):
+            return w4_codes[:, 2 * P * m : 2 * P * (m + 1)].bitcast(FP4X4), w4_plane[:, P * m : P * (m + 1)]
+
+        first_words = [gather_words(0, h, "first%d" % h) for h in range(2)]
+        for h in range(2):
+            for m in range(2):
+                multiply(first_words[h], 0, h, m, *w4_operand(m), True, False)
+
+        dw_operand = []
+        for m in range(2):
+            grouped = keep.tile([P, P, PACK], BF16, name="grouped%d" % m, tag="second%d" % m, align_bytes=64)
+            nc.scalar.copy(grouped[:], dw_raw[:, :, P * m : P * (m + 1)].rearrange("p j n -> p n j"))
+            codes = keep.tile([P, P], U32, name="dw_codes%d" % m, align_bytes=64)
+            plane = keep.tile([P, P], U8, name="dw_plane%d" % m, align_bytes=64)
+            nc.vector.quantize_mx(
+                out=codes[:].bitcast(FP8X4), scales=plane[:], in_=grouped[:].rearrange("p n j -> p (n j)")
+            )
+            dw_operand.append((codes[:].bitcast(FP8X4), plane[:]))
+            for h in range(2):
+                multiply(first_words[h], 0, h, m, *dw_operand[m], False, False)
+
+        for h in range(2):
+            words = gather_words(1, h, "second%d" % h)
+            for m in range(2):
+                multiply(words, 1, h, m, *w4_operand(m), False, False)
+                multiply(words, 1, h, m, *dw_operand[m], False, True)
+                result = keep.tile([P, N], F32, name="result%d%d" % (h, m))
+                nc.scalar.activation(result[:], banks[h][m][:], SILU, bias=bias[:, m : m + 1])
+                nc.sync.dma_start(out[P * m : P * (m + 1), h * N : (h + 1) * N], result[:])

@@ -34,31 +34,31 @@ def tile_list_tabbag_sum_silu_kernel(tc, tab, w4_words, w4_scales, dw, b, offs, 
         table_scales = keep.tile([P, T], U8, name="table_scales", align_bytes=64)
         w4_codes = keep.tile([P, 2 * M], U8, name="w4_codes", align_bytes=64)
         w4_plane = keep.tile([P, M], U8, name="w4_plane", align_bytes=64)
-        dw_raw = keep.tile([P, PACK, M], F32, name="dw_raw", align_bytes=64)
+        dw_raw = keep.tile([P, PACK, M], F32, name="dw_raw", tag="dw_then_words", align_bytes=64)
         bias = keep.tile([P, M // P], F32, name="bias")
         planes = [keep.tile([P, S], U8, name="plane%d" % g, align_bytes=64) for g in range(G)]
 
-        nc.vector.memset(w4_plane[:].bitcast(I32), 0)
+        nc.gpsimd.memset(w4_plane[:].bitcast(I32), 0)
         nc.vector.memset(table_scales[0:TOP, :].bitcast(I32), 0)
         for g in range(G):
             nc.vector.memset(planes[g][:].bitcast(I32), 0)
 
-        nc.sync.dma_start(offsets[:], offs)
-        nc.scalar.dma_start(
+        nc.sync.dma_start(
             table_scales[TOP:P, :].bitcast(I32),
             tab[0, 512 * T : 528 * T].rearrange("(q t) -> q t", q=BLOCKS).bitcast(I32),
         )
+        nc.sync.dma_start(offsets[:], offs)
         nc.sync.dma_start(
             table_words[:].bitcast(I32), tab[0, 0 : 512 * T].rearrange("(p t) -> p t", p=P).bitcast(I32)
         )
         for q in range(4):
-            nc.scalar.dma_start(
+            nc.gpsimd.dma_start(
                 w4_plane[32 * q : 32 * q + 4, :].bitcast(I32), w4_scales[0, 4 * q : 4 * q + 4, :].bitcast(I32)
             )
         nc.sync.dma_start(w4_codes[:].bitcast(I32), w4_words[0].bitcast(I32))
+        nc.sync.dma_start(dw_raw[:], dw.rearrange("(p j) n -> p j n", j=PACK))
         with nc.allow_non_contiguous_dma(reason="one bias value to a partition"):
             nc.sync.dma_start(bias[:], b.rearrange("(c p) -> p c", p=P))
-        nc.sync.dma_start(dw_raw[:], dw.rearrange("(p j) n -> p j n", j=PACK))
 
         for g, queue in enumerate((nc.scalar, nc.sync)):
             picked = keep.tile([P, S], U8, name="picked_scales%d" % g, align_bytes=64)
@@ -70,11 +70,9 @@ def tile_list_tabbag_sum_silu_kernel(tc, tab, w4_words, w4_scales, dw, b, offs, 
                     picked[TOP + 4 * q : TOP + 4 * q + 4, :].bitcast(I32),
                 )
 
-        def gather_words(g, h, tag):
-            picked = keep.tile([P, N], U32, name="picked_words%d%d" % (g, h), tag=tag, align_bytes=64)
+        def gather_words(picked, g, h):
             first = (g * S + h * N) // LANES
-            nc.vector.tensor_copy(picked[:], table_words[:].indirect(offsets[:, first : first + N // LANES]))
-            return picked
+            nc.vector.tensor_copy(picked, table_words[:].indirect(offsets[:, first : first + N // LANES]))
 
         banks = [[psum.tile([P, N], F32, name="bank%d%d" % (h, m)) for m in range(2)] for h in range(2)]
 
@@ -83,7 +81,7 @@ def tile_list_tabbag_sum_silu_kernel(tc, tab, w4_words, w4_scales, dw, b, offs, 
                 out=banks[h][m][:],
                 lhsT=codes,
                 lhsT_scale=plane,
-                rhs=words[:].bitcast(FP8X4),
+                rhs=words.bitcast(FP8X4),
                 rhs_scale=planes[g][:, h * N : (h + 1) * N],
                 start=start,
                 stop=stop,
@@ -92,29 +90,40 @@ def tile_list_tabbag_sum_silu_kernel(tc, tab, w4_words, w4_scales, dw, b, offs, 
         def w4_operand(m):
             return w4_codes[:, 2 * P * m : 2 * P * (m + 1)].bitcast(FP4X4), w4_plane[:, P * m : P * (m + 1)]
 
-        first_words = [gather_words(0, h, "first%d" % h) for h in range(2)]
+        first_words = keep.tile([P, S], U32, name="first_words", align_bytes=64)
+        for h in range(2):
+            gather_words(first_words[:, h * N : (h + 1) * N], 0, h)
+            for m in range(2):
+                multiply(first_words[:, h * N : (h + 1) * N], 0, h, m, *w4_operand(m), True, False)
+
+        grouped = keep.tile([P, M, PACK], BF16, name="grouped", align_bytes=64)
+        nc.scalar.copy(grouped[:], dw_raw[:].rearrange("p j n -> p n j"))
+        dw_codes = keep.tile([P, M], U32, name="dw_codes", align_bytes=64)
+        dw_plane = keep.tile([P, M], U8, name="dw_plane", align_bytes=64)
+        nc.vector.quantize_mx(
+            out=dw_codes[:].bitcast(FP8X4), scales=dw_plane[:], in_=grouped[:].rearrange("p n j -> p (n j)")
+        )
+
+        def dw_operand(m):
+            return dw_codes[:, P * m : P * (m + 1)].bitcast(FP8X4), dw_plane[:, P * m : P * (m + 1)]
+
         for h in range(2):
             for m in range(2):
-                multiply(first_words[h], 0, h, m, *w4_operand(m), True, False)
+                multiply(first_words[:, h * N : (h + 1) * N], 0, h, m, *dw_operand(m), False, False)
 
-        dw_operand = []
-        for m in range(2):
-            grouped = keep.tile([P, P, PACK], BF16, name="grouped%d" % m, tag="second%d" % m, align_bytes=64)
-            nc.scalar.copy(grouped[:], dw_raw[:, :, P * m : P * (m + 1)].rearrange("p j n -> p n j"))
-            codes = keep.tile([P, P], U32, name="dw_codes%d" % m, align_bytes=64)
-            plane = keep.tile([P, P], U8, name="dw_plane%d" % m, align_bytes=64)
-            nc.vector.quantize_mx(
-                out=codes[:].bitcast(FP8X4), scales=plane[:], in_=grouped[:].rearrange("p n j -> p (n j)")
-            )
-            dw_operand.append((codes[:].bitcast(FP8X4), plane[:]))
-            for h in range(2):
-                multiply(first_words[h], 0, h, m, *dw_operand[m], False, False)
-
+        second_words = keep.tile([P, S], U32, name="second_words", tag="dw_then_words", align_bytes=64)
         for h in range(2):
-            words = gather_words(1, h, "second%d" % h)
+            words = second_words[:, h * N : (h + 1) * N]
+            gather_words(words, 1, h)
             for m in range(2):
                 multiply(words, 1, h, m, *w4_operand(m), False, False)
-                multiply(words, 1, h, m, *dw_operand[m], False, True)
-                result = keep.tile([P, N], F32, name="result%d%d" % (h, m))
-                nc.scalar.activation(result[:], banks[h][m][:], SILU, bias=bias[:, m : m + 1])
-                nc.sync.dma_start(out[P * m : P * (m + 1), h * N : (h + 1) * N], result[:])
+                multiply(words, 1, h, m, *dw_operand(m), False, True)
+                pieces = 2 if (h, m) == (1, 1) else 1
+                width = N // pieces
+                for i in range(pieces):
+                    result = keep.tile([P, width], F32, name="result%d%d%d" % (h, m, i))
+                    nc.scalar.activation(
+                        result[:], banks[h][m][:, i * width : (i + 1) * width], SILU, bias=bias[:, m : m + 1]
+                    )
+                    first = h * N + i * width
+                    nc.sync.dma_start(out[P * m : P * (m + 1), first : first + width], result[:])

@@ -21,6 +21,8 @@ N = 512
 LANES = 16
 BLOCKS = 16
 TOP = P - BLOCKS
+WARM_M = 32
+WARM_PASSES = (4, 2)
 
 
 def tile_list_tabbag_sum_silu_kernel(tc, tab, w4_words, w4_scales, dw, b, offs, out):
@@ -48,9 +50,9 @@ def tile_list_tabbag_sum_silu_kernel(tc, tab, w4_words, w4_scales, dw, b, offs, 
             tab[0, 512 * T : 528 * T].rearrange("(q t) -> q t", q=BLOCKS).bitcast(I32),
         )
         nc.sync.dma_start(offsets[:], offs)
-        nc.sync.dma_start(
-            table_words[:].bitcast(I32), tab[0, 0 : 512 * T].rearrange("(p t) -> p t", p=P).bitcast(I32)
-        )
+        words_in_hbm = tab[0, 0 : 512 * T].rearrange("(p t) -> p t", p=P).bitcast(I32)
+        for cols in (slice(0, N), slice(N, T)):
+            nc.sync.dma_start(table_words[:, cols].bitcast(I32), words_in_hbm[:, cols])
         for q in range(4):
             nc.gpsimd.dma_start(
                 w4_plane[32 * q : 32 * q + 4, :].bitcast(I32), w4_scales[0, 4 * q : 4 * q + 4, :].bitcast(I32)
@@ -60,6 +62,7 @@ def tile_list_tabbag_sum_silu_kernel(tc, tab, w4_words, w4_scales, dw, b, offs, 
         with nc.allow_non_contiguous_dma(reason="one bias value to a partition"):
             nc.sync.dma_start(bias[:], b.rearrange("(c p) -> p c", p=P))
 
+        warm_bank = psum.tile([WARM_M, N], F32, name="warm_bank")
         for g, queue in enumerate((nc.scalar, nc.sync)):
             picked = keep.tile([P, S], U8, name="picked_scales%d" % g, align_bytes=64)
             cols = slice(g * S // LANES, (g + 1) * S // LANES)
@@ -68,6 +71,16 @@ def tile_list_tabbag_sum_silu_kernel(tc, tab, w4_words, w4_scales, dw, b, offs, 
                 queue.dma_start(
                     planes[g][32 * q : 32 * q + 4, :].bitcast(I32),
                     picked[TOP + 4 * q : TOP + 4 * q + 4, :].bitcast(I32),
+                )
+            for i in range(WARM_PASSES[g]):
+                nc.tensor.matmul_mx(
+                    out=warm_bank[:],
+                    lhsT=table_words[:, 0:WARM_M].bitcast(FP8X4),
+                    lhsT_scale=picked[:, 0:WARM_M],
+                    rhs=table_words[:, 0:N].bitcast(FP8X4),
+                    rhs_scale=picked[:, 0:N],
+                    start=True,
+                    stop=True,
                 )
 
         def gather_words(picked, g, h):

@@ -23,6 +23,8 @@ BLOCKS = 16
 TOP = P - BLOCKS
 WARM_M = 32
 WARM_PASSES = (4, 2)
+PIECE = 256
+FP4_N = 128
 
 
 def tile_list_tabbag_sum_silu_kernel(tc, tab, w4_words, w4_scales, dw, b, offs, out):
@@ -38,12 +40,12 @@ def tile_list_tabbag_sum_silu_kernel(tc, tab, w4_words, w4_scales, dw, b, offs, 
         w4_plane = keep.tile([P, M], U8, name="w4_plane", align_bytes=64)
         dw_raw = keep.tile([P, PACK, M], F32, name="dw_raw", tag="dw_then_words", align_bytes=64)
         bias = keep.tile([P, M // P], F32, name="bias")
-        planes = [keep.tile([P, S], U8, name="plane%d" % g, align_bytes=64) for g in range(G)]
+        planes = [keep.tile([P, G * N], U8, name="plane%d" % h, align_bytes=64) for h in range(2)]
 
         nc.gpsimd.memset(w4_plane[:].bitcast(I32), 0)
         nc.vector.memset(table_scales[0:TOP, :].bitcast(I32), 0)
-        for g in range(G):
-            nc.vector.memset(planes[g][:].bitcast(I32), 0)
+        for h in range(2):
+            nc.vector.memset(planes[h][:].bitcast(I32), 0)
 
         nc.sync.dma_start(
             table_scales[TOP:P, :].bitcast(I32),
@@ -57,57 +59,66 @@ def tile_list_tabbag_sum_silu_kernel(tc, tab, w4_words, w4_scales, dw, b, offs, 
             nc.gpsimd.dma_start(
                 w4_plane[32 * q : 32 * q + 4, :].bitcast(I32), w4_scales[0, 4 * q : 4 * q + 4, :].bitcast(I32)
             )
-        nc.sync.dma_start(w4_codes[:].bitcast(I32), w4_words[0].bitcast(I32))
         nc.sync.dma_start(dw_raw[:], dw.rearrange("(p j) n -> p j n", j=PACK))
+        nc.sync.dma_start(w4_codes[:].bitcast(I32), w4_words[0].bitcast(I32))
         with nc.allow_non_contiguous_dma(reason="one bias value to a partition"):
             nc.sync.dma_start(bias[:], b.rearrange("(c p) -> p c", p=P))
 
+        def gather(picked, table, g, h):
+            first = (g * S + h * N) // LANES
+            nc.vector.tensor_copy(
+                picked[:, g * N : (g + 1) * N], table[:].indirect(offsets[:, first : first + N // LANES])
+            )
+
         warm_bank = psum.tile([WARM_M, N], F32, name="warm_bank")
-        for g, queue in enumerate((nc.scalar, nc.sync)):
-            picked = keep.tile([P, S], U8, name="picked_scales%d" % g, align_bytes=64)
-            cols = slice(g * S // LANES, (g + 1) * S // LANES)
-            nc.vector.tensor_copy(picked[:], table_scales[:].indirect(offsets[:, cols]))
+        for h, queue in enumerate((nc.scalar, nc.sync)):
+            picked = keep.tile([P, G * N], U8, name="picked_scales%d" % h, align_bytes=64)
+            for g in range(G):
+                gather(picked, table_scales, g, h)
             for q in range(4):
                 queue.dma_start(
-                    planes[g][32 * q : 32 * q + 4, :].bitcast(I32),
+                    planes[h][32 * q : 32 * q + 4, :].bitcast(I32),
                     picked[TOP + 4 * q : TOP + 4 * q + 4, :].bitcast(I32),
                 )
-            for i in range(WARM_PASSES[g]):
+            for i in range(WARM_PASSES[h]):
                 nc.tensor.matmul_mx(
                     out=warm_bank[:],
                     lhsT=table_words[:, 0:WARM_M].bitcast(FP8X4),
-                    lhsT_scale=picked[:, 0:WARM_M],
+                    lhsT_scale=picked[:, N : N + WARM_M],
                     rhs=table_words[:, 0:N].bitcast(FP8X4),
-                    rhs_scale=picked[:, 0:N],
+                    rhs_scale=picked[:, N : 2 * N],
                     start=True,
                     stop=True,
                 )
 
-        def gather_words(picked, g, h):
-            first = (g * S + h * N) // LANES
-            nc.vector.tensor_copy(picked, table_words[:].indirect(offsets[:, first : first + N // LANES]))
-
-        banks = [[psum.tile([P, N], F32, name="bank%d%d" % (h, m)) for m in range(2)] for h in range(2)]
-
-        def multiply(words, g, h, m, codes, plane, start, stop):
+        def multiply(acc, weight, words, plane, first, width, start, stop):
+            cols = slice(first, first + width)
             nc.tensor.matmul_mx(
-                out=banks[h][m][:],
-                lhsT=codes,
-                lhsT_scale=plane,
-                rhs=words.bitcast(FP8X4),
-                rhs_scale=planes[g][:, h * N : (h + 1) * N],
+                out=acc,
+                lhsT=weight[0],
+                lhsT_scale=weight[1],
+                rhs=words[:, cols].bitcast(FP8X4),
+                rhs_scale=plane[:, cols],
                 start=start,
                 stop=stop,
             )
 
-        def w4_operand(m):
-            return w4_codes[:, 2 * P * m : 2 * P * (m + 1)].bitcast(FP4X4), w4_plane[:, P * m : P * (m + 1)]
+        def finish(acc, m, first, width):
+            result = keep.tile([P, width], F32, name="result%d_%d" % (m, first))
+            nc.scalar.activation(result[:], acc, SILU, bias=bias[:, m : m + 1])
+            nc.sync.dma_start(out[P * m : P * (m + 1), first : first + width], result[:])
 
-        first_words = keep.tile([P, S], U32, name="first_words", align_bytes=64)
-        for h in range(2):
-            gather_words(first_words[:, h * N : (h + 1) * N], 0, h)
+        w4 = [
+            (w4_codes[:, 2 * P * m : 2 * P * (m + 1)].bitcast(FP4X4), w4_plane[:, P * m : P * (m + 1)])
+            for m in range(2)
+        ]
+
+        early_words = keep.tile([P, G * N], U32, name="early_words", align_bytes=64)
+        early_banks = [psum.tile([P, N], F32, name="early_bank%d" % m) for m in range(2)]
+        for g in range(G):
+            gather(early_words, table_words, g, 0)
             for m in range(2):
-                multiply(first_words[:, h * N : (h + 1) * N], 0, h, m, *w4_operand(m), True, False)
+                multiply(early_banks[m][:], w4[m], early_words, planes[0], g * N, N, g == 0, False)
 
         grouped = keep.tile([P, M, PACK], BF16, name="grouped", align_bytes=64)
         nc.scalar.copy(grouped[:], dw_raw[:].rearrange("p j n -> p n j"))
@@ -116,27 +127,22 @@ def tile_list_tabbag_sum_silu_kernel(tc, tab, w4_words, w4_scales, dw, b, offs, 
         nc.vector.quantize_mx(
             out=dw_codes[:].bitcast(FP8X4), scales=dw_plane[:], in_=grouped[:].rearrange("p n j -> p (n j)")
         )
+        dwq = [(dw_codes[:, P * m : P * (m + 1)].bitcast(FP8X4), dw_plane[:, P * m : P * (m + 1)]) for m in range(2)]
 
-        def dw_operand(m):
-            return dw_codes[:, P * m : P * (m + 1)].bitcast(FP8X4), dw_plane[:, P * m : P * (m + 1)]
+        for m in range(2):
+            for g in range(G):
+                multiply(early_banks[m][:], dwq[m], early_words, planes[0], g * N, N, False, g == G - 1)
+            finish(early_banks[m][:], m, 0, N)
 
-        for h in range(2):
-            for m in range(2):
-                multiply(first_words[:, h * N : (h + 1) * N], 0, h, m, *dw_operand(m), False, False)
-
-        second_words = keep.tile([P, S], U32, name="second_words", tag="dw_then_words", align_bytes=64)
-        for h in range(2):
-            words = second_words[:, h * N : (h + 1) * N]
-            gather_words(words, 1, h)
-            for m in range(2):
-                multiply(words, 1, h, m, *w4_operand(m), False, False)
-                multiply(words, 1, h, m, *dw_operand(m), False, True)
-                pieces = 2 if (h, m) == (1, 1) else 1
-                width = N // pieces
-                for i in range(pieces):
-                    result = keep.tile([P, width], F32, name="result%d%d%d" % (h, m, i))
-                    nc.scalar.activation(
-                        result[:], banks[h][m][:, i * width : (i + 1) * width], SILU, bias=bias[:, m : m + 1]
-                    )
-                    first = h * N + i * width
-                    nc.sync.dma_start(out[P * m : P * (m + 1), first : first + width], result[:])
+        late_words = keep.tile([P, G * N], U32, name="late_words", tag="dw_then_words", align_bytes=64)
+        pieces = [(m, c) for m in range(2) for c in range(0, N, PIECE)]
+        late_banks = [psum.tile([P, PIECE], F32, name="late_bank%d_%d" % piece) for piece in pieces]
+        for g in range(G):
+            gather(late_words, table_words, g, 1)
+            for (m, c), bank in zip(pieces, late_banks):
+                multiply(bank[:], dwq[m], late_words, planes[1], g * N + c, PIECE, g == 0, False)
+                for s in range(0, PIECE, FP4_N):
+                    last = g == G - 1 and s + FP4_N == PIECE
+                    multiply(bank[:, s : s + FP4_N], w4[m], late_words, planes[1], g * N + c + s, FP4_N, False, last)
+                if g == G - 1:
+                    finish(bank[:], m, N + c, PIECE)

@@ -43,6 +43,10 @@ def tile_list_tabbag_sum_silu_kernel(tc, tab, w4_words, w4_scales, dw, b, offs, 
         planes = [keep.tile([P, G * N], U8, name="plane%d" % h, align_bytes=64) for h in range(2)]
 
         nc.gpsimd.memset(w4_plane[:].bitcast(I32), 0)
+        warm_in = keep.tile([P, 1], F32, name="warm_in")
+        warm_out = keep.tile([P, 1], F32, name="warm_out")
+        nc.vector.memset(warm_in[:], 0.0)
+        nc.scalar.activation(warm_out[:], warm_in[:], SILU)
         nc.vector.memset(table_scales[0:TOP, :].bitcast(I32), 0)
         for h in range(2):
             nc.vector.memset(planes[h][:].bitcast(I32), 0)
@@ -121,7 +125,9 @@ def tile_list_tabbag_sum_silu_kernel(tc, tab, w4_words, w4_scales, dw, b, offs, 
                 multiply(early_banks[m][:], w4[m], early_words, planes[0], g * N, N, g == 0, False)
 
         grouped = keep.tile([P, M, PACK], BF16, name="grouped", align_bytes=64)
-        nc.scalar.copy(grouped[:], dw_raw[:].rearrange("p j n -> p n j"))
+        nc.scalar.copy(
+            grouped[:].rearrange("p (c i) j -> p c j i", i=4), dw_raw[:].rearrange("p j (c i) -> p c j i", i=4)
+        )
         dw_codes = keep.tile([P, M], U32, name="dw_codes", align_bytes=64)
         dw_plane = keep.tile([P, M], U8, name="dw_plane", align_bytes=64)
         nc.vector.quantize_mx(

from contextlib import ExitStack

import concourse.mybir as mybir

G, K, M, T, S = 2, 512, 256, 4096, 1024
FLOPS = 2 * 2 * G * K * M * S

F32 = mybir.dt.float32
BF16 = mybir.dt.bfloat16
I32 = mybir.dt.int32
U32 = mybir.dt.uint32
U16 = mybir.dt.uint16
U8 = mybir.dt.uint8
FP8X4 = mybir.dt.float8_e4m3fn_x4
FP4X4 = mybir.dt.float4_e2m1fn_x4
SILU = mybir.ActivationFunctionType.Silu

P = 128
PACK = 4
N = 512
LANES = 16
BLOCKS = 16
TOP = P - BLOCKS
WARM_M = 32
WARM_PASSES = (4, 2)
PIECE = 256
FP4_N = 128


def tile_list_tabbag_sum_silu_kernel(tc, tab, w4_words, w4_scales, dw, b, offs, out):
    nc = tc.nc
    with ExitStack() as ctx:
        keep = ctx.enter_context(tc.tile_pool(name="keep", bufs=1))
        psum = ctx.enter_context(tc.psum_pool(name="psum", bufs=1))

        offsets = keep.tile([P, G * S // LANES], U16, name="offsets")
        table_words = keep.tile([P, T], U32, name="table_words", align_bytes=64)
        table_scales = keep.tile([P, T], U8, name="table_scales", align_bytes=64)
        w4_codes = keep.tile([P, 2 * M], U8, name="w4_codes", align_bytes=64)
        w4_plane = keep.tile([P, M], U8, name="w4_plane", align_bytes=64)
        dw_raw = keep.tile([P, PACK, M], F32, name="dw_raw", tag="dw_then_words", align_bytes=64)
        bias = keep.tile([P, M // P], F32, name="bias")
        planes = [keep.tile([P, G * N], U8, name="plane%d" % h, align_bytes=64) for h in range(2)]

        nc.gpsimd.memset(w4_plane[:].bitcast(I32), 0)
        warm_in = keep.tile([P, 1], F32, name="warm_in")
        warm_out = keep.tile([P, 1], F32, name="warm_out")
        nc.vector.memset(warm_in[:], 0.0)
        nc.scalar.activation(warm_out[:], warm_in[:], SILU)
        nc.vector.memset(table_scales[0:TOP, :].bitcast(I32), 0)
        for h in range(2):
            nc.vector.memset(planes[h][:].bitcast(I32), 0)

        nc.sync.dma_start(
            table_scales[TOP:P, :].bitcast(I32),
            tab[0, 512 * T : 528 * T].rearrange("(q t) -> q t", q=BLOCKS).bitcast(I32),
        )
        nc.sync.dma_start(offsets[:], offs)
        words_in_hbm = tab[0, 0 : 512 * T].rearrange("(p t) -> p t", p=P).bitcast(I32)
        for cols in (slice(0, N), slice(N, T)):
            nc.sync.dma_start(table_words[:, cols].bitcast(I32), words_in_hbm[:, cols])
        for q in range(4):
            nc.gpsimd.dma_start(
                w4_plane[32 * q : 32 * q + 4, :].bitcast(I32), w4_scales[0, 4 * q : 4 * q + 4, :].bitcast(I32)
            )
        nc.sync.dma_start(dw_raw[:], dw.rearrange("(p j) n -> p j n", j=PACK))
        nc.sync.dma_start(w4_codes[:].bitcast(I32), w4_words[0].bitcast(I32))
        with nc.allow_non_contiguous_dma(reason="one bias value to a partition"):
            nc.sync.dma_start(bias[:], b.rearrange("(c p) -> p c", p=P))

        def gather(picked, table, g, h):
            first = (g * S + h * N) // LANES
            nc.vector.tensor_copy(
                picked[:, g * N : (g + 1) * N], table[:].indirect(offsets[:, first : first + N // LANES])
            )

        warm_bank = psum.tile([WARM_M, N], F32, name="warm_bank")
        for h, queue in enumerate((nc.scalar, nc.sync)):
            picked = keep.tile([P, G * N], U8, name="picked_scales%d" % h, align_bytes=64)
            for g in range(G):
                gather(picked, table_scales, g, h)
            for q in range(4):
                queue.dma_start(
                    planes[h][32 * q : 32 * q + 4, :].bitcast(I32),
                    picked[TOP + 4 * q : TOP + 4 * q + 4, :].bitcast(I32),
                )
            for i in range(WARM_PASSES[h]):
                nc.tensor.matmul_mx(
                    out=warm_bank[:],
                    lhsT=table_words[:, 0:WARM_M].bitcast(FP8X4),
                    lhsT_scale=picked[:, N : N + WARM_M],
                    rhs=table_words[:, 0:N].bitcast(FP8X4),
                    rhs_scale=picked[:, N : 2 * N],
                    start=True,
                    stop=True,
                )

        def multiply(acc, weight, words, plane, first, width, start, stop):
            cols = slice(first, first + width)
            nc.tensor.matmul_mx(
                out=acc,
                lhsT=weight[0],
                lhsT_scale=weight[1],
                rhs=words[:, cols].bitcast(FP8X4),
                rhs_scale=plane[:, cols],
                start=start,
                stop=stop,
            )

        def finish(acc, m, first, width):
            result = keep.tile([P, width], F32, name="result%d_%d" % (m, first))
            nc.scalar.activation(result[:], acc, SILU, bias=bias[:, m : m + 1])
            nc.sync.dma_start(out[P * m : P * (m + 1), first : first + width], result[:])

        w4 = [
            (w4_codes[:, 2 * P * m : 2 * P * (m + 1)].bitcast(FP4X4), w4_plane[:, P * m : P * (m + 1)])
            for m in range(2)
        ]

        early_words = keep.tile([P, G * N], U32, name="early_words", align_bytes=64)
        early_banks = [psum.tile([P, N], F32, name="early_bank%d" % m) for m in range(2)]
        for g in range(G):
            gather(early_words, table_words, g, 0)
            for m in range(2):
                multiply(early_banks[m][:], w4[m], early_words, planes[0], g * N, N, g == 0, False)

        grouped = keep.tile([P, M, PACK], BF16, name="grouped", align_bytes=64)
        nc.scalar.copy(
            grouped[:].rearrange("p (c i) j -> p c j i", i=4), dw_raw[:].rearrange("p j (c i) -> p c j i", i=4)
        )
        dw_codes = keep.tile([P, M], U32, name="dw_codes", align_bytes=64)
        dw_plane = keep.tile([P, M], U8, name="dw_plane", align_bytes=64)
        nc.vector.quantize_mx(
            out=dw_codes[:].bitcast(FP8X4), scales=dw_plane[:], in_=grouped[:].rearrange("p n j -> p (n j)")
        )
        dwq = [(dw_codes[:, P * m : P * (m + 1)].bitcast(FP8X4), dw_plane[:, P * m : P * (m + 1)]) for m in range(2)]

        for m in range(2):
            for g in range(G):
                multiply(early_banks[m][:], dwq[m], early_words, planes[0], g * N, N, False, g == G - 1)
            finish(early_banks[m][:], m, 0, N)

        late_words = keep.tile([P, G * N], U32, name="late_words", tag="dw_then_words", align_bytes=64)
        pieces = [(m, c) for m in range(2) for c in range(0, N, PIECE)]
        late_banks = [psum.tile([P, PIECE], F32, name="late_bank%d_%d" % piece) for piece in pieces]
        for g in range(G):
            gather(late_words, table_words, g, 1)
            for (m, c), bank in zip(pieces, late_banks):
                multiply(bank[:], dwq[m], late_words, planes[1], g * N + c, PIECE, g == 0, False)
                for s in range(0, PIECE, FP4_N):
                    last = g == G - 1 and s + FP4_N == PIECE
                    multiply(bank[:, s : s + FP4_N], w4[m], late_words, planes[1], g * N + c + s, FP4_N, False, last)
                if g == G - 1:
                    finish(bank[:], m, N + c, PIECE)
